import numpy as np
import ml_dtypes

BF16 = ml_dtypes.bfloat16


def bf(x):
    return np.asarray(x, np.float32).astype(BF16)


def f32(x):
    return np.asarray(x, np.float32)


def f64(x):
    return np.asarray(x).astype(np.float64)


def striped(idx):
    return np.tile(idx.reshape(-1, 16).T, (8, 1))


S, K, M, N = 1024, 128, 256, 512


def setup_inputs():
    return {"table": bf(np.random.standard_normal((S, K))), "w": bf(np.random.standard_normal((K, M)) / np.sqrt(K)), "b": f32(0.5 * np.random.standard_normal((M, 1))), "offs": striped(np.random.permutation(S)[:N])}


def reference(table, w, b, offs):
    idx = offs[:16].T.reshape(-1)
    x = f64(table)[idx].T
    y = f64(w).T @ x
    return np.tanh(y + f64(b))

@@ -1,0 +1,59 @@
+import concourse.mybir as mybir
+from concourse.masks import make_identity
+
+BF16 = mybir.dt.bfloat16
+F32 = mybir.dt.float32
+U16 = mybir.dt.uint16
+TANH = mybir.ActivationFunctionType.Tanh
+
+P = 128
+S = 1024
+K = 128
+M = 256
+N = 512
+
+FLOPS = 2 * K * M * N
+
+
+def tile_gather_matmul_kernel(tc, table, w, b, offs, out):
+    nc = tc.nc
+    with (
+        tc.tile_pool(name="held", bufs=1) as held,
+        tc.tile_pool(name="results", bufs=2) as results,
+        tc.psum_pool(name="flips", bufs=2) as flips,
+        tc.psum_pool(name="products", bufs=2) as products,
+    ):
+        offsets = held.tile([P, N // 16], U16, name="offsets")
+        nc.sync.dma_start(offsets[:], offs)
+
+        samples = held.tile([P, S // P, K], BF16, name="samples")
+        nc.sync.dma_start(samples[:], table.rearrange("(a p) k -> p a k", p=P))
+
+        weights = held.tile([K, M], BF16, name="weights")
+        nc.scalar.dma_start(weights[:], w)
+
+        bias = held.tile([P, M // P], F32, name="bias")
+        with nc.allow_non_contiguous_dma(reason="one float32 to a partition"):
+            nc.scalar.dma_start(bias[:], b.rearrange("(a p) o -> p (a o)", p=P))
+
+        identity = held.tile([P, P], BF16, name="identity")
+        make_identity(nc, identity[:])
+
+        window = held.tile([K, S], BF16, name="window")
+        for a in range(S // P):
+            flipped = flips.tile([K, P], BF16, name="flipped")
+            nc.tensor.transpose(flipped[:], samples[:, a, :], identity[:])
+            nc.vector.tensor_copy(window[:, a * P : (a + 1) * P], flipped[:])
+
+        for m in range(M // P):
+            product = products.tile([P, N], F32, name="product")
+            nc.tensor.matmul(
+                product[:],
+                weights[:, m * P : (m + 1) * P],
+                window[:].indirect(offsets[:]),
+                start=True,
+                stop=True,
+            )
+            result = results.tile([P, N], F32, name="result")
+            nc.scalar.activation(result[:], product[:], TANH, bias=bias[:, m : m + 1])
+            nc.sync.dma_start(out[m * P : (m + 1) * P, :], result[:])

@@ -14,46 +14,61 @@ N = 512
 
 FLOPS = 2 * K * M * N
 
+CHUNK = 256
+PIECE = 256
+
 
 def tile_gather_matmul_kernel(tc, table, w, b, offs, out):
     nc = tc.nc
     with (
         tc.tile_pool(name="held", bufs=1) as held,
-        tc.tile_pool(name="results", bufs=2) as results,
-        tc.psum_pool(name="flips", bufs=2) as flips,
-        tc.psum_pool(name="products", bufs=2) as products,
+        tc.psum_pool(name="flips", bufs=S // CHUNK) as flips,
+        tc.psum_pool(name="products", bufs=(M // P) * (N // PIECE)) as products,
     ):
+        chunks = []
+        for c in range(S // CHUNK):
+            samples = held.tile([P, CHUNK // P, K], BF16, name=f"samples{c}")
+            queue = nc.sync if c % 2 == 0 else nc.scalar
+            queue.dma_start(
+                samples[:],
+                table[c * CHUNK : (c + 1) * CHUNK, :].rearrange("(a p) k -> p a k", p=P),
+            )
+            chunks.append(samples)
+
         offsets = held.tile([P, N // 16], U16, name="offsets")
         nc.sync.dma_start(offsets[:], offs)
-
-        samples = held.tile([P, S // P, K], BF16, name="samples")
-        nc.sync.dma_start(samples[:], table.rearrange("(a p) k -> p a k", p=P))
 
         weights = held.tile([K, M], BF16, name="weights")
         nc.scalar.dma_start(weights[:], w)
 
         bias = held.tile([P, M // P], F32, name="bias")
         with nc.allow_non_contiguous_dma(reason="one float32 to a partition"):
-            nc.scalar.dma_start(bias[:], b.rearrange("(a p) o -> p (a o)", p=P))
+            nc.sync.dma_start(bias[:], b.rearrange("(a p) o -> p (a o)", p=P))
 
         identity = held.tile([P, P], BF16, name="identity")
         make_identity(nc, identity[:])
 
+        scratch = held.tile([P, 1], F32, name="scratch")
+        nc.vector.memset(scratch[:], 0.0)
+        nc.scalar.activation(scratch[:], scratch[:], TANH)
+
         window = held.tile([K, S], BF16, name="window")
-        for a in range(S // P):
-            flipped = flips.tile([K, P], BF16, name="flipped")
-            nc.tensor.transpose(flipped[:], samples[:, a, :], identity[:])
-            nc.vector.tensor_copy(window[:, a * P : (a + 1) * P], flipped[:])
+        for c in range(S // CHUNK):
+            flipped = flips.tile([K, CHUNK], BF16, name="flipped")
+            for a in range(CHUNK // P):
+                nc.tensor.transpose(flipped[:, a * P : (a + 1) * P], chunks[c][:, a, :], identity[:])
+            nc.vector.tensor_copy(window[:, c * CHUNK : (c + 1) * CHUNK], flipped[:])
 
         for m in range(M // P):
-            product = products.tile([P, N], F32, name="product")
-            nc.tensor.matmul(
-                product[:],
-                weights[:, m * P : (m + 1) * P],
-                window[:].indirect(offsets[:]),
-                start=True,
-                stop=True,
-            )
-            result = results.tile([P, N], F32, name="result")
-            nc.scalar.activation(result[:], product[:], TANH, bias=bias[:, m : m + 1])
-            nc.sync.dma_start(out[m * P : (m + 1) * P, :], result[:])
+            for q in range(N // PIECE):
+                product = products.tile([P, PIECE], F32, name="product")
+                nc.tensor.matmul(
+                    product[:],
+                    weights[:, m * P : (m + 1) * P],
+                    window[:].indirect(offsets[:, q * PIECE // 16 : (q + 1) * PIECE // 16]),
+                    start=True,
+                    stop=True,
+                )
+                result = held.tile([P, PIECE], F32, name=f"result{m}{q}")
+                nc.scalar.activation(result[:], product[:], TANH, bias=bias[:, m : m + 1])
+                nc.sync.dma_start(out[m * P : (m + 1) * P, q * PIECE : (q + 1) * PIECE], result[:])

@@ -16,13 +16,15 @@ FLOPS = 2 * K * M * N
 
 CHUNK = 256
 PIECE = 256
+WARM = 2
 
 
 def tile_gather_matmul_kernel(tc, table, w, b, offs, out):
     nc = tc.nc
     with (
         tc.tile_pool(name="held", bufs=1) as held,
-        tc.psum_pool(name="flips", bufs=S // CHUNK) as flips,
+        tc.psum_pool(name="idle", bufs=1) as idle,
+        tc.psum_pool(name="flips", bufs=3) as flips,
         tc.psum_pool(name="products", bufs=(M // P) * (N // PIECE)) as products,
     ):
         chunks = []
@@ -51,6 +53,16 @@ def tile_gather_matmul_kernel(tc, table, w, b, offs, out):
         scratch = held.tile([P, 1], F32, name="scratch")
         nc.vector.memset(scratch[:], 0.0)
         nc.scalar.activation(scratch[:], scratch[:], TANH)
+
+        zeros = held.tile([P, 512], BF16, name="zeros")
+        nc.vector.memset(zeros[:], 0.0)
+        unread = idle.tile([P, 512], F32, name="unread")
+
+        def idle_matmul():
+            nc.tensor.matmul(unread[:], zeros[:, 0:P], zeros[:], start=True, stop=True)
+
+        for i in range(WARM):
+            idle_matmul()
 
         window = held.tile([K, S], BF16, name="window")
         for c in range(S // CHUNK):

@@ -65,11 +65,12 @@ def tile_gather_matmul_kernel(tc, table, w, b, offs, out):
             idle_matmul()
 
         window = held.tile([K, S], BF16, name="window")
-        for c in range(S // CHUNK):
-            flipped = flips.tile([K, CHUNK], BF16, name="flipped")
-            for a in range(CHUNK // P):
-                nc.tensor.transpose(flipped[:, a * P : (a + 1) * P], chunks[c][:, a, :], identity[:])
-            nc.vector.tensor_copy(window[:, c * CHUNK : (c + 1) * CHUNK], flipped[:])
+        blocks = [chunks[c][:, a, :] for c in range(S // CHUNK) for a in range(CHUNK // P)]
+        for first, end in ((0, 4), (4, 6), (6, 8)):
+            flipped = flips.tile([K, 2 * CHUNK], BF16, name="flipped")
+            for t in range(first, end):
+                nc.tensor.transpose(flipped[:, (t - first) * P : (t - first + 1) * P], blocks[t], identity[:])
+            nc.vector.tensor_copy(window[:, first * P : end * P], flipped[:, 0 : (end - first) * P])
 
         for m in range(M // P):
             for q in range(N // PIECE):

@@ -50,16 +50,15 @@ def tile_gather_matmul_kernel(tc, table, w, b, offs, out):
         identity = held.tile([P, P], BF16, name="identity")
         make_identity(nc, identity[:])
 
-        scratch = held.tile([P, 1], F32, name="scratch")
-        nc.vector.memset(scratch[:], 0.0)
-        nc.scalar.activation(scratch[:], scratch[:], TANH)
-
-        zeros = held.tile([P, 512], BF16, name="zeros")
+        zeros = held.tile([P, P], BF16, name="zeros")
         nc.vector.memset(zeros[:], 0.0)
+        scratch = held.tile([P, 1], F32, name="scratch")
+        nc.scalar.activation(scratch[:], zeros[:, 0:1], TANH)
+
         unread = idle.tile([P, 512], F32, name="unread")
 
         def idle_matmul():
-            nc.tensor.matmul(unread[:], zeros[:, 0:P], zeros[:], start=True, stop=True)
+            nc.tensor.matmul(unread[:], zeros[:], zeros[:, 0:1].to_broadcast([P, 512]), start=True, stop=True)
 
         for i in range(WARM):
             idle_matmul()

import concourse.mybir as mybir
from concourse.masks import make_identity

BF16 = mybir.dt.bfloat16
F32 = mybir.dt.float32
U16 = mybir.dt.uint16
TANH = mybir.ActivationFunctionType.Tanh

P = 128
S = 1024
K = 128
M = 256
N = 512

FLOPS = 2 * K * M * N

CHUNK = 256
PIECE = 256
WARM = 2


def tile_gather_matmul_kernel(tc, table, w, b, offs, out):
    nc = tc.nc
    with (
        tc.tile_pool(name="held", bufs=1) as held,
        tc.psum_pool(name="idle", bufs=1) as idle,
        tc.psum_pool(name="flips", bufs=3) as flips,
        tc.psum_pool(name="products", bufs=(M // P) * (N // PIECE)) as products,
    ):
        chunks = []
        for c in range(S // CHUNK):
            samples = held.tile([P, CHUNK // P, K], BF16, name=f"samples{c}")
            queue = nc.sync if c % 2 == 0 else nc.scalar
            queue.dma_start(
                samples[:],
                table[c * CHUNK : (c + 1) * CHUNK, :].rearrange("(a p) k -> p a k", p=P),
            )
            chunks.append(samples)

        offsets = held.tile([P, N // 16], U16, name="offsets")
        nc.sync.dma_start(offsets[:], offs)

        weights = held.tile([K, M], BF16, name="weights")
        nc.scalar.dma_start(weights[:], w)

        bias = held.tile([P, M // P], F32, name="bias")
        with nc.allow_non_contiguous_dma(reason="one float32 to a partition"):
            nc.sync.dma_start(bias[:], b.rearrange("(a p) o -> p (a o)", p=P))

        identity = held.tile([P, P], BF16, name="identity")
        make_identity(nc, identity[:])

        zeros = held.tile([P, P], BF16, name="zeros")
        nc.vector.memset(zeros[:], 0.0)
        scratch = held.tile([P, 1], F32, name="scratch")
        nc.scalar.activation(scratch[:], zeros[:, 0:1], TANH)

        unread = idle.tile([P, 512], F32, name="unread")

        def idle_matmul():
            nc.tensor.matmul(unread[:], zeros[:], zeros[:, 0:1].to_broadcast([P, 512]), start=True, stop=True)

        for i in range(WARM):
            idle_matmul()

        window = held.tile([K, S], BF16, name="window")
        blocks = [chunks[c][:, a, :] for c in range(S // CHUNK) for a in range(CHUNK // P)]
        for first, end in ((0, 4), (4, 6), (6, 8)):
            flipped = flips.tile([K, 2 * CHUNK], BF16, name="flipped")
            for t in range(first, end):
                nc.tensor.transpose(flipped[:, (t - first) * P : (t - first + 1) * P], blocks[t], identity[:])
            nc.vector.tensor_copy(window[:, first * P : end * P], flipped[:, 0 : (end - first) * P])

        for m in range(M // P):
            for q in range(N // PIECE):
                product = products.tile([P, PIECE], F32, name="product")
                nc.tensor.matmul(
                    product[:],
                    weights[:, m * P : (m + 1) * P],
                    window[:].indirect(offsets[:, q * PIECE // 16 : (q + 1) * PIECE // 16]),
                    start=True,
                    stop=True,
                )
                result = held.tile([P, PIECE], F32, name=f"result{m}{q}")
                nc.scalar.activation(result[:], product[:], TANH, bias=bias[:, m : m + 1])
                nc.sync.dma_start(out[m * P : (m + 1) * P, q * PIECE : (q + 1) * PIECE], result[:])
